import numpy as np
import ml_dtypes


def mxq(x, axis, fmt="e4m3"):
    dtype, down = {"e4m3": (ml_dtypes.float8_e4m3fn, 7), "e5m2": (ml_dtypes.float8_e5m2, 14)}[fmt]
    v = np.moveaxis(np.asarray(x, np.float32).astype(ml_dtypes.bfloat16).astype(np.float64), axis, -1)
    blocks = v.reshape(v.shape[:-1] + (-1, 32))
    amax = np.abs(blocks).max(-1, keepdims=True)
    byte = np.maximum(np.where(amax > 0, np.frexp(amax)[1] - 1 + 127, 0) - down, 1)
    scale = np.exp2(byte - 127.0)
    codes = (blocks / scale).astype(np.float32).astype(dtype).astype(np.float64)
    return np.moveaxis((codes * scale).reshape(v.shape), -1, axis)


WIDE = False


def mx_kscale(k):
    if not WIDE:
        return np.ones(k)
    levels = np.array([10, -10, 5, -5, 0])
    if k % 512:
        return np.exp2(np.random.permutation(np.resize(levels, k // 32))).repeat(32)
    a = np.empty((k // 512, 16))
    for p in range(k // 512):
        a[p, :8] = np.random.permutation(np.resize(levels, 8))
        for g in range(8):
            far = levels[np.abs(levels - a[p, g]) >= 10]
            a[p, g + 8] = far[np.random.randint(len(far))]
    return np.exp2(a.ravel()).repeat(32)


def f64(x):
    return np.asarray(x).astype(np.float64)


def striped(idx):
    return np.tile(idx.reshape(-1, 16).T, (8, 1)).astype(np.uint16)


def unstriped(offs):
    return offs[:16].T.reshape(-1).astype(np.int64)


def striped8(idx):
    return np.concatenate([x.reshape(-1, 16).T for x in idx]).astype(np.uint16)


def runs(offs, k):
    lists = np.stack([offs[16 * r : 16 * r + 16].T.reshape(-1) for r in range(8)]).astype(np.int64)
    return lists[np.arange(k) % 512 // 64]


def pack_weight(w):
    k, n = w.shape
    w = f64(np.asarray(w, np.float32).astype(ml_dtypes.bfloat16)).reshape(k // 32, 32, n)
    amax = np.abs(w).max(1)
    byte = np.clip(np.where(amax > 0, np.frexp(amax)[1] - 1 + 127 - 7, 1), 1, 254)
    scaled = (w * np.exp2(127.0 - byte)[:, None, :]).reshape(k, n).astype(np.float32)
    words = np.ascontiguousarray(scaled.reshape(k // 512, 128, 4, n).transpose(0, 1, 3, 2)).astype(ml_dtypes.float8_e4m3fn).view(np.uint8)
    return words, np.ascontiguousarray(byte.astype(np.uint8).reshape(k // 512, 16, n))


def unpack_weight(words, scales):
    g, p, n, _ = words.shape
    vals = np.ascontiguousarray(words).view(ml_dtypes.float8_e4m3fn).astype(np.float64) * np.repeat(np.exp2(scales.astype(np.float64) - 127.0), 8, axis=1)[..., None]
    return vals.transpose(0, 1, 3, 2).reshape(g * 512, n)


K, T, S, G, H, W = 512, 1024, 512, 2048, 512, 256


def setup_inputs():
    n = np.random.standard_normal
    s = mx_kscale(K)[:, None]
    packed_xT = pack_weight(n((K, T)) * s)
    packed_dT = pack_weight(n((K, G)) / s)
    perm = np.stack([np.random.permutation(S) for _ in range(8)])
    return {
        "x_words": packed_xT[0],
        "x_scales": packed_xT[1],
        "d_words": packed_dT[0],
        "d_scales": packed_dT[1],
        "gs": (np.random.uniform(0.5, 1.5, (K, 1)) * s).astype(np.float32),
        "offs": striped(np.random.permutation(T)[:S]),
        "k1": striped8(np.random.randint(0, G, (8, H))),
        "n1": striped8(perm[:, :W]),
        "n2": striped8(perm[:, W:]),
        "k2": striped8(np.random.randint(0, G, (8, H))),
        "n3": striped8(np.stack([np.random.permutation(S) for _ in range(8)])),
        "n4": striped8(np.stack([np.random.permutation(S) for _ in range(8)])),
    }


def reference(x_words, x_scales, d_words, d_scales, gs, offs, k1, n1, n2, k2, n3, n4):
    d_k2 = unpack_weight(d_words, d_scales)[np.arange(K)[:, None], runs(k2, K)]
    d_k1 = unpack_weight(d_words, d_scales)[np.arange(K)[:, None], runs(k1, K)]
    xq = unpack_weight(x_words, x_scales)[:, unstriped(offs)]
    h = 0.0625 * (d_k1.T @ xq)
    pa = h[np.arange(H)[:, None], runs(n1, H)]
    pb = h[np.arange(H)[:, None], runs(n2, H)]
    ra = np.maximum(pa, pb)
    ds = h.copy()
    ds[np.arange(H)[:, None], runs(n1, H)] = ra
    z = f64(gs) * ds
    h2 = 0.0625 * ((d_k2.T @ mxq(z, 0, "e4m3")))
    st = np.maximum(h2, h2[np.arange(H)[:, None], runs(n3, H)])
    return np.minimum(st, st[np.arange(H)[:, None], runs(n4, H)])

@@ -1,0 +1,226 @@
+from contextlib import ExitStack
+
+import concourse.mybir as mybir
+
+K, T, S, G, H, W = 512, 1024, 512, 2048, 512, 256
+FLOPS = 2 * K * H * S + 2 * H * H * S
+
+F32 = mybir.dt.float32
+BF16 = mybir.dt.bfloat16
+I32 = mybir.dt.int32
+U32 = mybir.dt.uint32
+U16 = mybir.dt.uint16
+U8 = mybir.dt.uint8
+FP8X4 = mybir.dt.float8_e4m3fn_x4
+COPY = mybir.ActivationFunctionType.Copy
+MAX = mybir.AluOpType.max
+MIN = mybir.AluOpType.min
+
+P = 128
+PACK = 4
+HALF = S // 2
+SIXTEENTH = 0.0625
+
+
+def tile_picked_codefillhopmn_none_p_kernel(
+    tc, x_words, x_scales, d_words, d_scales, gs, offs, k1, n1, n2, k2, n3, n4, out
+):
+    nc = tc.nc
+    with ExitStack() as ctx:
+        lists = ctx.enter_context(tc.tile_pool(name="lists", bufs=1))
+        keep = ctx.enter_context(tc.tile_pool(name="keep", bufs=1))
+        psum = ctx.enter_context(tc.psum_pool(name="psum", bufs=1))
+
+        def tile(name, shape, dtype, tag=None):
+            return keep.tile(shape, dtype, name=name, tag=tag or name, align_bytes=64)
+
+        def load_list(name, dram):
+            held = lists.tile(list(dram.shape), U16, name=name)
+            nc.sync.dma_start(held[:], dram)
+            return held
+
+        d_byte_table = tile("d_byte_table", [P, G], U8)
+        x_byte_table = tile("x_byte_table", [P, T], U8)
+        d_word_table = tile("d_word_table", [P, G], U32)
+        x_word_table = tile("x_word_table", [P, T], U32)
+        placed1 = tile("placed1", [P, H + S], U8)
+        placed2 = tile("placed2", [P, H], U8)
+        gs_raw = tile("gs_raw", [P, PACK], F32)
+        gs16 = tile("gs16", [P, PACK], F32)
+
+        nc.gpsimd.dma_start(gs_raw[:], gs.rearrange("(p t) o -> p (t o)", t=PACK))
+        nc.gpsimd.memset(placed1[:].bitcast(I32), 0)
+        nc.gpsimd.memset(placed2[:].bitcast(I32), 0)
+
+        def load_bytes(table, rows):
+            words = rows.bitcast(I32)
+            nc.sync.dma_start(table[:].bitcast(I32), words.unsqueeze(1).to_broadcast([16, 8, words.shape[1]]))
+
+        k1_list = load_list("k1_list", k1)
+        load_bytes(d_byte_table, d_scales[0])
+        offs_list = load_list("offs_list", offs)
+        load_bytes(x_byte_table, x_scales[0])
+        nc.sync.dma_start(x_word_table[:].bitcast(I32), x_words[0].rearrange("p n t -> p (n t)").bitcast(I32))
+        k2_list = load_list("k2_list", k2)
+        n1_list = load_list("n1_list", n1)
+        nc.sync.dma_start(d_word_table[:].bitcast(I32), d_words[0].rearrange("p n t -> p (n t)").bitcast(I32))
+        n2_list = load_list("n2_list", n2)
+        n3_list = load_list("n3_list", n3)
+        n4_list = load_list("n4_list", n4)
+
+        nc.scalar.activation(gs16[:], gs_raw[:], COPY, scale=SIXTEENTH)
+
+        def place_rows(placed, picked):
+            for j in range(4):
+                nc.sync.dma_start(placed[j:P:32, :].bitcast(I32), picked[8 * j : P : 32, :].bitcast(I32))
+
+        def deal(dealt, natural, t0, t1):
+            nc.vector.tensor_copy(
+                dealt[:, t0 * P : t1 * P].rearrange("p (t m) -> p t m", m=P),
+                natural.rearrange("p (m t) -> p t m", t=PACK)[:, t0:t1, :],
+            )
+
+        picked1 = tile("picked1", [P, H + S], U8, "picked_bytes")
+        x_codes = tile("x_codes", [P, S], U32)
+        w1_picked = tile("w1_picked", [P, H], U32)
+        w1_codes = tile("w1_codes", [P, H], U32)
+        w2_codes = tile("w2_codes", [P, H], U32)
+        w1_scales = tile("w1_scales", [P, H], U8)
+        w2_scales = tile("w2_scales", [P, H], U8)
+
+        nc.vector.tensor_copy(picked1[:, :H], d_byte_table[:].indirect(k1_list[:]))
+        nc.vector.tensor_copy(picked1[:, H:], x_byte_table[:].indirect(offs_list[:]))
+        place_rows(placed1, picked1)
+        nc.vector.tensor_copy(x_codes[:], x_word_table[:].indirect(offs_list[:]))
+        nc.vector.tensor_copy(w1_picked[:], d_word_table[:].indirect(k1_list[:]))
+        deal(w1_codes, w1_picked[:], 0, PACK)
+        deal(w1_scales, placed1[:, :H], 0, 1)
+        deal(w1_scales, placed1[:, :H], 1, PACK)
+        picked2 = tile("picked2", [P, H], U8, "picked_bytes")
+        nc.vector.tensor_copy(picked2[:], d_byte_table[:].indirect(k2_list[:]))
+        place_rows(placed2, picked2)
+
+        banks = [psum.tile([P, S], F32, name="bank%d" % b) for b in range(8)]
+
+        def product(bank, cols, w_codes, w_scales, t, codes, scales):
+            rows = slice(t * P, (t + 1) * P)
+            nc.tensor.matmul_mx(
+                out=bank[:, cols],
+                lhsT=w_codes[:, rows].bitcast(FP8X4),
+                lhsT_scale=w_scales[:, rows],
+                rhs=codes.bitcast(FP8X4),
+                rhs_scale=scales,
+                start=True,
+                stop=True,
+            )
+
+        halves = [slice(0, HALF), slice(HALF, S)]
+        ds = [tile("ds%d" % t, [P, S], F32) for t in range(PACK)]
+        h2 = [tile("h2_%d" % t, [P, 2 * S], F32) for t in range(PACK)]
+        st = [tile("st%d" % t, [P, 2 * S], F32) for t in range(PACK)]
+        res = [tile("res%d" % t, [P, S], F32) for t in range(PACK)]
+        z = tile("z", [P, S, PACK], BF16)
+        z_codes = tile("z_codes", [P, S], U32)
+        z_scales = tile("z_scales", [P, S], U8)
+        x_plane = placed1[:, H:]
+
+        for c, cols in enumerate(halves):
+            product(banks[c], cols, w1_codes, w1_scales, 0, x_codes[:, cols], x_plane[:, cols])
+            nc.scalar.activation(ds[0][:, cols], banks[c][:, cols], COPY)
+        for t in range(1, PACK):
+            product(banks[t + 1], slice(0, S), w1_codes, w1_scales, t, x_codes[:], x_plane)
+            nc.scalar.activation(ds[t][:], banks[t + 1][:], COPY)
+
+        def pa(t):
+            return h2[t][:, S : S + W]
+
+        def pb(t):
+            return h2[t][:, S + W :]
+
+        def fetch_a(t):
+            nc.vector.tensor_copy(pa(t), ds[t][:].indirect(n1_list[:]))
+
+        def fetch_b(t):
+            nc.vector.tensor_copy(pb(t), ds[t][:].indirect(n2_list[:]))
+
+        ra_last = tile("ra_last", [P, W], F32, "after_scatter")
+
+        def ra(t):
+            return ra_last[:] if t == PACK - 1 else pa(t)
+
+        def larger(t):
+            nc.vector.tensor_tensor(ra(t), pa(t), pb(t), MAX)
+
+        def put_back(t):
+            nc.vector.tensor_copy(ds[t][:].indirect(n1_list[:]), ra(t))
+            for cols in halves:
+                nc.scalar.activation(z[:, cols, t], ds[t][:, cols], COPY, scale=gs16[:, t : t + 1])
+
+        fetch_a(0)
+        fetch_b(0)
+        for t in range(1, PACK):
+            fetch_a(t)
+            larger(t - 1)
+            fetch_b(t)
+            if t >= 2:
+                put_back(t - 2)
+        larger(PACK - 1)
+        put_back(PACK - 2)
+        put_back(PACK - 1)
+        deal(w2_scales, placed2[:], 0, PACK)
+        w2_picked = tile("w2_picked", [P, H], U32, "after_scatter")
+        nc.vector.tensor_copy(w2_picked[:], d_word_table[:].indirect(k2_list[:]))
+        nc.vector.quantize_mx(
+            out=z_codes[:, halves[0]].bitcast(FP8X4),
+            scales=z_scales[:, halves[0]],
+            in_=z[:, halves[0], :].rearrange("p n t -> p (n t)"),
+        )
+        deal(w2_codes, w2_picked[:], 0, 1)
+        nc.vector.quantize_mx(
+            out=z_codes[:, halves[1]].bitcast(FP8X4),
+            scales=z_scales[:, halves[1]],
+            in_=z[:, halves[1], :].rearrange("p n t -> p (n t)"),
+        )
+        deal(w2_codes, w2_picked[:], 1, PACK)
+
+        for c, cols in enumerate(halves):
+            product(banks[5 + c], cols, w2_codes, w2_scales, 0, z_codes[:, cols], z_scales[:, cols])
+            nc.scalar.activation(h2[0][:, cols], banks[5 + c][:, cols], COPY, scale=SIXTEENTH)
+        for t in range(1, PACK):
+            bank = banks[(6 + t) % 8]
+            product(bank, slice(0, S), w2_codes, w2_scales, t, z_codes[:], z_scales[:])
+            nc.scalar.activation(h2[t][:, :S], bank[:], COPY, scale=SIXTEENTH)
+
+        out_rows = out.rearrange("(p t) n -> t p n", t=PACK)
+
+        def fetch3(t):
+            nc.vector.tensor_copy(st[t][:, S:], h2[t][:].indirect(n3_list[:]))
+
+        def larger3(t):
+            nc.vector.tensor_tensor(st[t][:, :S], h2[t][:, :S], st[t][:, S:], MAX)
+
+        def fetch4(t, a, b):
+            nc.vector.tensor_copy(res[t][:, a:b], st[t][:].indirect(n4_list[:, a // 16 : b // 16]))
+
+        def smaller4(t, a, b):
+            nc.vector.tensor_tensor(res[t][:, a:b], res[t][:, a:b], st[t][:, a:b], MIN)
+            nc.sync.dma_start(out_rows[t][:, a:b], res[t][:, a:b])
+
+        fetch3(0)
+        fetch3(1)
+        larger3(0)
+        fetch3(2)
+        fetch4(0, 0, S)
+        larger3(1)
+        smaller4(0, 0, S)
+        fetch3(3)
+        fetch4(1, 0, S)
+        larger3(2)
+        smaller4(1, 0, S)
+        larger3(3)
+        fetch4(2, 0, S)
+        fetch4(3, 0, HALF)
+        smaller4(2, 0, S)
+        fetch4(3, HALF, S)
+        smaller4(3, 0, HALF)
+        smaller4(3, HALF, S)

@@ -49,17 +49,17 @@ def tile_picked_codefillhopmn_none_p_kernel(
         gs16 = tile("gs16", [P, PACK], F32)
 
         nc.gpsimd.dma_start(gs_raw[:], gs.rearrange("(p t) o -> p (t o)", t=PACK))
-        nc.gpsimd.memset(placed1[:].bitcast(I32), 0)
-        nc.gpsimd.memset(placed2[:].bitcast(I32), 0)
+        nc.vector.memset(placed1[:].bitcast(I32), 0)
+        nc.vector.memset(placed2[:].bitcast(I32), 0)
 
         def load_bytes(table, rows):
             words = rows.bitcast(I32)
             nc.sync.dma_start(table[:].bitcast(I32), words.unsqueeze(1).to_broadcast([16, 8, words.shape[1]]))
 
-        k1_list = load_list("k1_list", k1)
-        load_bytes(d_byte_table, d_scales[0])
         offs_list = load_list("offs_list", offs)
         load_bytes(x_byte_table, x_scales[0])
+        k1_list = load_list("k1_list", k1)
+        load_bytes(d_byte_table, d_scales[0])
         nc.sync.dma_start(x_word_table[:].bitcast(I32), x_words[0].rearrange("p n t -> p (n t)").bitcast(I32))
         k2_list = load_list("k2_list", k2)
         n1_list = load_list("n1_list", n1)
@@ -76,38 +76,41 @@ def tile_picked_codefillhopmn_none_p_kernel(
 
         def deal(dealt, natural, t0, t1):
             nc.vector.tensor_copy(
-                dealt[:, t0 * P : t1 * P].rearrange("p (t m) -> p t m", m=P),
+                dealt.rearrange("p (t m) -> p t m", m=P),
                 natural.rearrange("p (m t) -> p t m", t=PACK)[:, t0:t1, :],
             )
 
         picked1 = tile("picked1", [P, H + S], U8, "picked_bytes")
         x_codes = tile("x_codes", [P, S], U32)
         w1_picked = tile("w1_picked", [P, H], U32)
-        w1_codes = tile("w1_codes", [P, H], U32)
-        w2_codes = tile("w2_codes", [P, H], U32)
+        w1_codes = tile("w1_codes", [P, P], U32)
         w1_scales = tile("w1_scales", [P, H], U8)
-        w2_scales = tile("w2_scales", [P, H], U8)
+        w2_scales = tile("w2_scales", [P, P], U8)
 
-        nc.vector.tensor_copy(picked1[:, :H], d_byte_table[:].indirect(k1_list[:]))
         nc.vector.tensor_copy(picked1[:, H:], x_byte_table[:].indirect(offs_list[:]))
-        place_rows(placed1, picked1)
+        nc.vector.tensor_copy(picked1[:, :H], d_byte_table[:].indirect(k1_list[:]))
+        place_rows(placed1[:], picked1)
         nc.vector.tensor_copy(x_codes[:], x_word_table[:].indirect(offs_list[:]))
         nc.vector.tensor_copy(w1_picked[:], d_word_table[:].indirect(k1_list[:]))
-        deal(w1_codes, w1_picked[:], 0, PACK)
-        deal(w1_scales, placed1[:, :H], 0, 1)
-        deal(w1_scales, placed1[:, :H], 1, PACK)
-        picked2 = tile("picked2", [P, H], U8, "picked_bytes")
+        deal(w1_codes[:], w1_picked[:], 0, 1)
+        deal(w1_scales[:, :P], placed1[:, :H], 0, 1)
+        w1_codes_rest = tile("w1_codes_rest", [P, H - P], U32, "picked_bytes")
+        deal(w1_codes_rest[:], w1_picked[:], 1, PACK)
+        deal(w1_scales[:, P:], placed1[:, :H], 1, PACK)
+        picked2 = tile("picked2", [P, H], U8, "w1_picked")
         nc.vector.tensor_copy(picked2[:], d_byte_table[:].indirect(k2_list[:]))
-        place_rows(placed2, picked2)
+        place_rows(placed2[:], picked2)
 
         banks = [psum.tile([P, S], F32, name="bank%d" % b) for b in range(8)]
 
-        def product(bank, cols, w_codes, w_scales, t, codes, scales):
-            rows = slice(t * P, (t + 1) * P)
+        def rows(t):
+            return slice(t * P, (t + 1) * P)
+
+        def product(bank, cols, w_codes, w_scales, codes, scales):
             nc.tensor.matmul_mx(
                 out=bank[:, cols],
-                lhsT=w_codes[:, rows].bitcast(FP8X4),
-                lhsT_scale=w_scales[:, rows],
+                lhsT=w_codes.bitcast(FP8X4),
+                lhsT_scale=w_scales,
                 rhs=codes.bitcast(FP8X4),
                 rhs_scale=scales,
                 start=True,
@@ -115,20 +118,21 @@ def tile_picked_codefillhopmn_none_p_kernel(
             )
 
         halves = [slice(0, HALF), slice(HALF, S)]
+        chunks = [slice(0, HALF), slice(HALF, HALF + P), slice(HALF + P, S)]
         ds = [tile("ds%d" % t, [P, S], F32) for t in range(PACK)]
         h2 = [tile("h2_%d" % t, [P, 2 * S], F32) for t in range(PACK)]
         st = [tile("st%d" % t, [P, 2 * S], F32) for t in range(PACK)]
         res = [tile("res%d" % t, [P, S], F32) for t in range(PACK)]
-        z = tile("z", [P, S, PACK], BF16)
+        z = [tile("z%d" % c, [P, cols.stop - cols.start, PACK], BF16) for c, cols in enumerate(chunks)]
         z_codes = tile("z_codes", [P, S], U32)
         z_scales = tile("z_scales", [P, S], U8)
         x_plane = placed1[:, H:]
 
         for c, cols in enumerate(halves):
-            product(banks[c], cols, w1_codes, w1_scales, 0, x_codes[:, cols], x_plane[:, cols])
+            product(banks[c], cols, w1_codes[:], w1_scales[:, rows(0)], x_codes[:, cols], x_plane[:, cols])
             nc.scalar.activation(ds[0][:, cols], banks[c][:, cols], COPY)
         for t in range(1, PACK):
-            product(banks[t + 1], slice(0, S), w1_codes, w1_scales, t, x_codes[:], x_plane)
+            product(banks[t + 1], slice(0, S), w1_codes_rest[:, rows(t - 1)], w1_scales[:, rows(t)], x_codes[:], x_plane)
             nc.scalar.activation(ds[t][:], banks[t + 1][:], COPY)
 
         def pa(t):
@@ -153,8 +157,8 @@ def tile_picked_codefillhopmn_none_p_kernel(
 
         def put_back(t):
             nc.vector.tensor_copy(ds[t][:].indirect(n1_list[:]), ra(t))
-            for cols in halves:
-                nc.scalar.activation(z[:, cols, t], ds[t][:, cols], COPY, scale=gs16[:, t : t + 1])
+            for c, cols in enumerate(chunks):
+                nc.scalar.activation(z[c][:, :, t], ds[t][:, cols], COPY, scale=gs16[:, t : t + 1])
 
         fetch_a(0)
         fetch_b(0)
@@ -167,28 +171,37 @@ def tile_picked_codefillhopmn_none_p_kernel(
         larger(PACK - 1)
         put_back(PACK - 2)
         put_back(PACK - 1)
-        deal(w2_scales, placed2[:], 0, PACK)
+        deal(w2_scales[:], placed2[:], 0, 1)
         w2_picked = tile("w2_picked", [P, H], U32, "after_scatter")
         nc.vector.tensor_copy(w2_picked[:], d_word_table[:].indirect(k2_list[:]))
-        nc.vector.quantize_mx(
-            out=z_codes[:, halves[0]].bitcast(FP8X4),
-            scales=z_scales[:, halves[0]],
-            in_=z[:, halves[0], :].rearrange("p n t -> p (n t)"),
-        )
-        deal(w2_codes, w2_picked[:], 0, 1)
-        nc.vector.quantize_mx(
-            out=z_codes[:, halves[1]].bitcast(FP8X4),
-            scales=z_scales[:, halves[1]],
-            in_=z[:, halves[1], :].rearrange("p n t -> p (n t)"),
-        )
-        deal(w2_codes, w2_picked[:], 1, PACK)
 
-        for c, cols in enumerate(halves):
-            product(banks[5 + c], cols, w2_codes, w2_scales, 0, z_codes[:, cols], z_scales[:, cols])
+        def quantise(c):
+            cols = chunks[c]
+            nc.vector.quantize_mx(
+                out=z_codes[:, cols].bitcast(FP8X4),
+                scales=z_scales[:, cols],
+                in_=z[c][:].rearrange("p n t -> p (n t)"),
+            )
+
+        quantise(0)
+        quantise(1)
+        w2_codes = tile("w2_codes", [P, P], U32, "z0")
+        deal(w2_codes[:], w2_picked[:], 0, 1)
+        quantise(2)
+        w2_codes_rest = tile("w2_codes_rest", [P, H - P], U32, "z1")
+        deal(w2_codes_rest[:], w2_picked[:], 1, PACK)
+        w2_scales_rest = tile("w2_scales_rest", [P, H - P], U8, "z2")
+        deal(w2_scales_rest[:], placed2[:], 1, PACK)
+
+        for c, cols in enumerate(chunks):
+            product(banks[5 + c], cols, w2_codes[:], w2_scales[:], z_codes[:, cols], z_scales[:, cols])
             nc.scalar.activation(h2[0][:, cols], banks[5 + c][:, cols], COPY, scale=SIXTEENTH)
-        for t in range(1, PACK):
-            bank = banks[(6 + t) % 8]
-            product(bank, slice(0, S), w2_codes, w2_scales, t, z_codes[:], z_scales[:])
+        for c, cols in enumerate(halves):
+            product(banks[c], cols, w2_codes_rest[:, rows(0)], w2_scales_rest[:, rows(0)], z_codes[:, cols], z_scales[:, cols])
+            nc.scalar.activation(h2[1][:, cols], banks[c][:, cols], COPY, scale=SIXTEENTH)
+        for t in range(2, PACK):
+            bank = banks[t]
+            product(bank, slice(0, S), w2_codes_rest[:, rows(t - 1)], w2_scales_rest[:, rows(t - 1)], z_codes[:], z_scales[:])
             nc.scalar.activation(h2[t][:, :S], bank[:], COPY, scale=SIXTEENTH)
 
         out_rows = out.rearrange("(p t) n -> t p n", t=PACK)
@@ -217,10 +230,10 @@ def tile_picked_codefillhopmn_none_p_kernel(
         fetch4(1, 0, S)
         larger3(2)
         smaller4(1, 0, S)
-        larger3(3)
         fetch4(2, 0, S)
-        fetch4(3, 0, HALF)
+        larger3(3)
         smaller4(2, 0, S)
+        fetch4(3, 0, HALF)
         fetch4(3, HALF, S)
         smaller4(3, 0, HALF)
         smaller4(3, HALF, S)

@@ -46,8 +46,9 @@ def tile_picked_codefillhopmn_none_p_kernel(
         placed1 = tile("placed1", [P, H + S], U8)
         placed2 = tile("placed2", [P, H], U8)
         gs_raw = tile("gs_raw", [P, PACK], F32)
-        gs16 = tile("gs16", [P, PACK], F32)
 
+        nc.vector.memset(d_byte_table[:, : G // 2].bitcast(I32), 0)
+        nc.gpsimd.memset(d_byte_table[:, G // 2 :].bitcast(I32), 0)
         nc.gpsimd.dma_start(gs_raw[:], gs.rearrange("(p t) o -> p (t o)", t=PACK))
         nc.vector.memset(placed1[:].bitcast(I32), 0)
         nc.vector.memset(placed2[:].bitcast(I32), 0)
@@ -59,7 +60,7 @@ def tile_picked_codefillhopmn_none_p_kernel(
         offs_list = load_list("offs_list", offs)
         load_bytes(x_byte_table, x_scales[0])
         k1_list = load_list("k1_list", k1)
-        load_bytes(d_byte_table, d_scales[0])
+        nc.scalar.dma_start(d_byte_table[0:P:8, :].bitcast(I32), d_scales[0].bitcast(I32))
         nc.sync.dma_start(x_word_table[:].bitcast(I32), x_words[0].rearrange("p n t -> p (n t)").bitcast(I32))
         k2_list = load_list("k2_list", k2)
         n1_list = load_list("n1_list", n1)
@@ -68,11 +69,11 @@ def tile_picked_codefillhopmn_none_p_kernel(
         n3_list = load_list("n3_list", n3)
         n4_list = load_list("n4_list", n4)
 
-        nc.scalar.activation(gs16[:], gs_raw[:], COPY, scale=SIXTEENTH)
 
-        def place_rows(placed, picked):
+        def place_rows(placed, picked, odd_queue):
             for j in range(4):
-                nc.sync.dma_start(placed[j:P:32, :].bitcast(I32), picked[8 * j : P : 32, :].bitcast(I32))
+                queue = nc.sync if j % 2 == 0 else odd_queue
+                queue.dma_start(placed[j:P:32, :].bitcast(I32), picked[8 * j : P : 32, :].bitcast(I32))
 
         def deal(dealt, natural, t0, t1):
             nc.vector.tensor_copy(
@@ -83,23 +84,21 @@ def tile_picked_codefillhopmn_none_p_kernel(
         picked1 = tile("picked1", [P, H + S], U8, "picked_bytes")
         x_codes = tile("x_codes", [P, S], U32)
         w1_picked = tile("w1_picked", [P, H], U32)
-        w1_codes = tile("w1_codes", [P, P], U32)
+        w1_codes = tile("w1_codes", [P, H], U32)
         w1_scales = tile("w1_scales", [P, H], U8)
         w2_scales = tile("w2_scales", [P, P], U8)
 
         nc.vector.tensor_copy(picked1[:, H:], x_byte_table[:].indirect(offs_list[:]))
         nc.vector.tensor_copy(picked1[:, :H], d_byte_table[:].indirect(k1_list[:]))
-        place_rows(placed1[:], picked1)
+        place_rows(placed1[:], picked1, nc.scalar)
         nc.vector.tensor_copy(x_codes[:], x_word_table[:].indirect(offs_list[:]))
         nc.vector.tensor_copy(w1_picked[:], d_word_table[:].indirect(k1_list[:]))
-        deal(w1_codes[:], w1_picked[:], 0, 1)
+        deal(w1_codes[:], w1_picked[:], 0, PACK)
         deal(w1_scales[:, :P], placed1[:, :H], 0, 1)
-        w1_codes_rest = tile("w1_codes_rest", [P, H - P], U32, "picked_bytes")
-        deal(w1_codes_rest[:], w1_picked[:], 1, PACK)
         deal(w1_scales[:, P:], placed1[:, :H], 1, PACK)
-        picked2 = tile("picked2", [P, H], U8, "w1_picked")
+        picked2 = tile("picked2", [P, H], U8, "picked_bytes")
         nc.vector.tensor_copy(picked2[:], d_byte_table[:].indirect(k2_list[:]))
-        place_rows(placed2[:], picked2)
+        place_rows(placed2[:], picked2, nc.sync)
 
         banks = [psum.tile([P, S], F32, name="bank%d" % b) for b in range(8)]
 
@@ -129,11 +128,11 @@ def tile_picked_codefillhopmn_none_p_kernel(
         x_plane = placed1[:, H:]
 
         for c, cols in enumerate(halves):
-            product(banks[c], cols, w1_codes[:], w1_scales[:, rows(0)], x_codes[:, cols], x_plane[:, cols])
-            nc.scalar.activation(ds[0][:, cols], banks[c][:, cols], COPY)
+            product(banks[c], cols, w1_codes[:, rows(0)], w1_scales[:, rows(0)], x_codes[:, cols], x_plane[:, cols])
+            nc.scalar.activation(ds[0][:, cols], banks[c][:, cols], COPY, scale=SIXTEENTH)
         for t in range(1, PACK):
-            product(banks[t + 1], slice(0, S), w1_codes_rest[:, rows(t - 1)], w1_scales[:, rows(t)], x_codes[:], x_plane)
-            nc.scalar.activation(ds[t][:], banks[t + 1][:], COPY)
+            product(banks[t + 1], slice(0, S), w1_codes[:, rows(t)], w1_scales[:, rows(t)], x_codes[:], x_plane)
+            nc.scalar.activation(ds[t][:], banks[t + 1][:], COPY, scale=SIXTEENTH)
 
         def pa(t):
             return h2[t][:, S : S + W]
@@ -150,7 +149,7 @@ def tile_picked_codefillhopmn_none_p_kernel(
         ra_last = tile("ra_last", [P, W], F32, "after_scatter")
 
         def ra(t):
-            return ra_last[:] if t == PACK - 1 else pa(t)
+            return ra_last[:] if t == PACK - 2 else pa(t)
 
         def larger(t):
             nc.vector.tensor_tensor(ra(t), pa(t), pb(t), MAX)
@@ -158,7 +157,7 @@ def tile_picked_codefillhopmn_none_p_kernel(
         def put_back(t):
             nc.vector.tensor_copy(ds[t][:].indirect(n1_list[:]), ra(t))
             for c, cols in enumerate(chunks):
-                nc.scalar.activation(z[c][:, :, t], ds[t][:, cols], COPY, scale=gs16[:, t : t + 1])
+                nc.scalar.activation(z[c][:, :, t], ds[t][:, cols], COPY, scale=gs_raw[:, t : t + 1])
 
         fetch_a(0)
         fetch_b(0)
@@ -183,10 +182,10 @@ def tile_picked_codefillhopmn_none_p_kernel(
                 in_=z[c][:].rearrange("p n t -> p (n t)"),
             )
 
+        w2_codes = tile("w2_codes", [P, P], U32)
+        deal(w2_codes[:], w2_picked[:], 0, 1)
         quantise(0)
         quantise(1)
-        w2_codes = tile("w2_codes", [P, P], U32, "z0")
-        deal(w2_codes[:], w2_picked[:], 0, 1)
         quantise(2)
         w2_codes_rest = tile("w2_codes_rest", [P, H - P], U32, "z1")
         deal(w2_codes_rest[:], w2_picked[:], 1, PACK)

@@ -76,9 +76,10 @@ def tile_picked_codefillhopmn_none_p_kernel(
                 queue.dma_start(placed[j:P:32, :].bitcast(I32), picked[8 * j : P : 32, :].bitcast(I32))
 
         def deal(dealt, natural, t0, t1):
+            run = 4 if natural.dtype == U32 else 16
             nc.vector.tensor_copy(
-                dealt.rearrange("p (t m) -> p t m", m=P),
-                natural.rearrange("p (m t) -> p t m", t=PACK)[:, t0:t1, :],
+                dealt.rearrange("p (t c i) -> p c t i", c=P // run, i=run),
+                natural.rearrange("p (c i t) -> p c t i", i=run, t=PACK)[:, :, t0:t1, :],
             )
 
         picked1 = tile("picked1", [P, H + S], U8, "picked_bytes")

from contextlib import ExitStack

import concourse.mybir as mybir

K, T, S, G, H, W = 512, 1024, 512, 2048, 512, 256
FLOPS = 2 * K * H * S + 2 * H * H * S

F32 = mybir.dt.float32
BF16 = mybir.dt.bfloat16
I32 = mybir.dt.int32
U32 = mybir.dt.uint32
U16 = mybir.dt.uint16
U8 = mybir.dt.uint8
FP8X4 = mybir.dt.float8_e4m3fn_x4
COPY = mybir.ActivationFunctionType.Copy
MAX = mybir.AluOpType.max
MIN = mybir.AluOpType.min

P = 128
PACK = 4
HALF = S // 2
SIXTEENTH = 0.0625


def tile_picked_codefillhopmn_none_p_kernel(
    tc, x_words, x_scales, d_words, d_scales, gs, offs, k1, n1, n2, k2, n3, n4, out
):
    nc = tc.nc
    with ExitStack() as ctx:
        lists = ctx.enter_context(tc.tile_pool(name="lists", bufs=1))
        keep = ctx.enter_context(tc.tile_pool(name="keep", bufs=1))
        psum = ctx.enter_context(tc.psum_pool(name="psum", bufs=1))

        def tile(name, shape, dtype, tag=None):
            return keep.tile(shape, dtype, name=name, tag=tag or name, align_bytes=64)

        def load_list(name, dram):
            held = lists.tile(list(dram.shape), U16, name=name)
            nc.sync.dma_start(held[:], dram)
            return held

        d_byte_table = tile("d_byte_table", [P, G], U8)
        x_byte_table = tile("x_byte_table", [P, T], U8)
        d_word_table = tile("d_word_table", [P, G], U32)
        x_word_table = tile("x_word_table", [P, T], U32)
        placed1 = tile("placed1", [P, H + S], U8)
        placed2 = tile("placed2", [P, H], U8)
        gs_raw = tile("gs_raw", [P, PACK], F32)

        nc.vector.memset(d_byte_table[:, : G // 2].bitcast(I32), 0)
        nc.gpsimd.memset(d_byte_table[:, G // 2 :].bitcast(I32), 0)
        nc.gpsimd.dma_start(gs_raw[:], gs.rearrange("(p t) o -> p (t o)", t=PACK))
        nc.vector.memset(placed1[:].bitcast(I32), 0)
        nc.vector.memset(placed2[:].bitcast(I32), 0)

        def load_bytes(table, rows):
            words = rows.bitcast(I32)
            nc.sync.dma_start(table[:].bitcast(I32), words.unsqueeze(1).to_broadcast([16, 8, words.shape[1]]))

        offs_list = load_list("offs_list", offs)
        load_bytes(x_byte_table, x_scales[0])
        k1_list = load_list("k1_list", k1)
        nc.scalar.dma_start(d_byte_table[0:P:8, :].bitcast(I32), d_scales[0].bitcast(I32))
        nc.sync.dma_start(x_word_table[:].bitcast(I32), x_words[0].rearrange("p n t -> p (n t)").bitcast(I32))
        k2_list = load_list("k2_list", k2)
        n1_list = load_list("n1_list", n1)
        nc.sync.dma_start(d_word_table[:].bitcast(I32), d_words[0].rearrange("p n t -> p (n t)").bitcast(I32))
        n2_list = load_list("n2_list", n2)
        n3_list = load_list("n3_list", n3)
        n4_list = load_list("n4_list", n4)


        def place_rows(placed, picked, odd_queue):
            for j in range(4):
                queue = nc.sync if j % 2 == 0 else odd_queue
                queue.dma_start(placed[j:P:32, :].bitcast(I32), picked[8 * j : P : 32, :].bitcast(I32))

        def deal(dealt, natural, t0, t1):
            run = 4 if natural.dtype == U32 else 16
            nc.vector.tensor_copy(
                dealt.rearrange("p (t c i) -> p c t i", c=P // run, i=run),
                natural.rearrange("p (c i t) -> p c t i", i=run, t=PACK)[:, :, t0:t1, :],
            )

        picked1 = tile("picked1", [P, H + S], U8, "picked_bytes")
        x_codes = tile("x_codes", [P, S], U32)
        w1_picked = tile("w1_picked", [P, H], U32)
        w1_codes = tile("w1_codes", [P, H], U32)
        w1_scales = tile("w1_scales", [P, H], U8)
        w2_scales = tile("w2_scales", [P, P], U8)

        nc.vector.tensor_copy(picked1[:, H:], x_byte_table[:].indirect(offs_list[:]))
        nc.vector.tensor_copy(picked1[:, :H], d_byte_table[:].indirect(k1_list[:]))
        place_rows(placed1[:], picked1, nc.scalar)
        nc.vector.tensor_copy(x_codes[:], x_word_table[:].indirect(offs_list[:]))
        nc.vector.tensor_copy(w1_picked[:], d_word_table[:].indirect(k1_list[:]))
        deal(w1_codes[:], w1_picked[:], 0, PACK)
        deal(w1_scales[:, :P], placed1[:, :H], 0, 1)
        deal(w1_scales[:, P:], placed1[:, :H], 1, PACK)
        picked2 = tile("picked2", [P, H], U8, "picked_bytes")
        nc.vector.tensor_copy(picked2[:], d_byte_table[:].indirect(k2_list[:]))
        place_rows(placed2[:], picked2, nc.sync)

        banks = [psum.tile([P, S], F32, name="bank%d" % b) for b in range(8)]

        def rows(t):
            return slice(t * P, (t + 1) * P)

        def product(bank, cols, w_codes, w_scales, codes, scales):
            nc.tensor.matmul_mx(
                out=bank[:, cols],
                lhsT=w_codes.bitcast(FP8X4),
                lhsT_scale=w_scales,
                rhs=codes.bitcast(FP8X4),
                rhs_scale=scales,
                start=True,
                stop=True,
            )

        halves = [slice(0, HALF), slice(HALF, S)]
        chunks = [slice(0, HALF), slice(HALF, HALF + P), slice(HALF + P, S)]
        ds = [tile("ds%d" % t, [P, S], F32) for t in range(PACK)]
        h2 = [tile("h2_%d" % t, [P, 2 * S], F32) for t in range(PACK)]
        st = [tile("st%d" % t, [P, 2 * S], F32) for t in range(PACK)]
        res = [tile("res%d" % t, [P, S], F32) for t in range(PACK)]
        z = [tile("z%d" % c, [P, cols.stop - cols.start, PACK], BF16) for c, cols in enumerate(chunks)]
        z_codes = tile("z_codes", [P, S], U32)
        z_scales = tile("z_scales", [P, S], U8)
        x_plane = placed1[:, H:]

        for c, cols in enumerate(halves):
            product(banks[c], cols, w1_codes[:, rows(0)], w1_scales[:, rows(0)], x_codes[:, cols], x_plane[:, cols])
            nc.scalar.activation(ds[0][:, cols], banks[c][:, cols], COPY, scale=SIXTEENTH)
        for t in range(1, PACK):
            product(banks[t + 1], slice(0, S), w1_codes[:, rows(t)], w1_scales[:, rows(t)], x_codes[:], x_plane)
            nc.scalar.activation(ds[t][:], banks[t + 1][:], COPY, scale=SIXTEENTH)

        def pa(t):
            return h2[t][:, S : S + W]

        def pb(t):
            return h2[t][:, S + W :]

        def fetch_a(t):
            nc.vector.tensor_copy(pa(t), ds[t][:].indirect(n1_list[:]))

        def fetch_b(t):
            nc.vector.tensor_copy(pb(t), ds[t][:].indirect(n2_list[:]))

        ra_last = tile("ra_last", [P, W], F32, "after_scatter")

        def ra(t):
            return ra_last[:] if t == PACK - 2 else pa(t)

        def larger(t):
            nc.vector.tensor_tensor(ra(t), pa(t), pb(t), MAX)

        def put_back(t):
            nc.vector.tensor_copy(ds[t][:].indirect(n1_list[:]), ra(t))
            for c, cols in enumerate(chunks):
                nc.scalar.activation(z[c][:, :, t], ds[t][:, cols], COPY, scale=gs_raw[:, t : t + 1])

        fetch_a(0)
        fetch_b(0)
        for t in range(1, PACK):
            fetch_a(t)
            larger(t - 1)
            fetch_b(t)
            if t >= 2:
                put_back(t - 2)
        larger(PACK - 1)
        put_back(PACK - 2)
        put_back(PACK - 1)
        deal(w2_scales[:], placed2[:], 0, 1)
        w2_picked = tile("w2_picked", [P, H], U32, "after_scatter")
        nc.vector.tensor_copy(w2_picked[:], d_word_table[:].indirect(k2_list[:]))

        def quantise(c):
            cols = chunks[c]
            nc.vector.quantize_mx(
                out=z_codes[:, cols].bitcast(FP8X4),
                scales=z_scales[:, cols],
                in_=z[c][:].rearrange("p n t -> p (n t)"),
            )

        w2_codes = tile("w2_codes", [P, P], U32)
        deal(w2_codes[:], w2_picked[:], 0, 1)
        quantise(0)
        quantise(1)
        quantise(2)
        w2_codes_rest = tile("w2_codes_rest", [P, H - P], U32, "z1")
        deal(w2_codes_rest[:], w2_picked[:], 1, PACK)
        w2_scales_rest = tile("w2_scales_rest", [P, H - P], U8, "z2")
        deal(w2_scales_rest[:], placed2[:], 1, PACK)

        for c, cols in enumerate(chunks):
            product(banks[5 + c], cols, w2_codes[:], w2_scales[:], z_codes[:, cols], z_scales[:, cols])
            nc.scalar.activation(h2[0][:, cols], banks[5 + c][:, cols], COPY, scale=SIXTEENTH)
        for c, cols in enumerate(halves):
            product(banks[c], cols, w2_codes_rest[:, rows(0)], w2_scales_rest[:, rows(0)], z_codes[:, cols], z_scales[:, cols])
            nc.scalar.activation(h2[1][:, cols], banks[c][:, cols], COPY, scale=SIXTEENTH)
        for t in range(2, PACK):
            bank = banks[t]
            product(bank, slice(0, S), w2_codes_rest[:, rows(t - 1)], w2_scales_rest[:, rows(t - 1)], z_codes[:], z_scales[:])
            nc.scalar.activation(h2[t][:, :S], bank[:], COPY, scale=SIXTEENTH)

        out_rows = out.rearrange("(p t) n -> t p n", t=PACK)

        def fetch3(t):
            nc.vector.tensor_copy(st[t][:, S:], h2[t][:].indirect(n3_list[:]))

        def larger3(t):
            nc.vector.tensor_tensor(st[t][:, :S], h2[t][:, :S], st[t][:, S:], MAX)

        def fetch4(t, a, b):
            nc.vector.tensor_copy(res[t][:, a:b], st[t][:].indirect(n4_list[:, a // 16 : b // 16]))

        def smaller4(t, a, b):
            nc.vector.tensor_tensor(res[t][:, a:b], res[t][:, a:b], st[t][:, a:b], MIN)
            nc.sync.dma_start(out_rows[t][:, a:b], res[t][:, a:b])

        fetch3(0)
        fetch3(1)
        larger3(0)
        fetch3(2)
        fetch4(0, 0, S)
        larger3(1)
        smaller4(0, 0, S)
        fetch3(3)
        fetch4(1, 0, S)
        larger3(2)
        smaller4(1, 0, S)
        fetch4(2, 0, S)
        larger3(3)
        smaller4(2, 0, S)
        fetch4(3, 0, HALF)
        fetch4(3, HALF, S)
        smaller4(3, 0, HALF)
        smaller4(3, HALF, S)
